import numpy as np
import ml_dtypes


def mxq(x, axis, fmt="e4m3"):
    dtype, down = {"e4m3": (ml_dtypes.float8_e4m3fn, 7), "e5m2": (ml_dtypes.float8_e5m2, 14)}[fmt]
    v = np.moveaxis(np.asarray(x, np.float32).astype(ml_dtypes.bfloat16).astype(np.float64), axis, -1)
    blocks = v.reshape(v.shape[:-1] + (-1, 32))
    amax = np.abs(blocks).max(-1, keepdims=True)
    byte = np.maximum(np.where(amax > 0, np.frexp(amax)[1] - 1 + 127, 0) - down, 1)
    scale = np.exp2(byte - 127.0)
    codes = (blocks / scale).astype(np.float32).astype(dtype).astype(np.float64)
    return np.moveaxis((codes * scale).reshape(v.shape), -1, axis)


WIDE = False


def mx_kscale(k):
    if not WIDE:
        return np.ones(k)
    levels = np.array([30, -30])
    if k % 512:
        return np.exp2(np.random.permutation(np.resize(levels, k // 32))).repeat(32)
    a = np.empty((k // 512, 16))
    for p in range(k // 512):
        a[p, :8] = np.random.permutation(np.resize(levels, 8))
        for g in range(8):
            far = levels[np.abs(levels - a[p, g]) >= 10]
            a[p, g + 8] = far[np.random.randint(len(far))]
    return np.exp2(a.ravel()).repeat(32)


def f64(x):
    return np.asarray(x).astype(np.float64)


K, L, M, N = 1536, 1536, 256, 1024


def setup_inputs():
    n = np.random.standard_normal
    s1 = mx_kscale(K)[:, None]
    s2 = mx_kscale(L)[:, None]
    m1, m2 = np.exp(0.5 * n((1, M))), np.exp(0.5 * n((1, N)))
    return {
        "x": (n((K, M)) / np.sqrt(K) * s1).astype(np.float32),
        "xt": (n((K, N)) / s1).astype(np.float32),
        "g": (m1 * n((L, M)) / np.sqrt(L) * s2).astype(np.float32),
        "gt": (m2 * n((L, N)) / s2).astype(np.float32),
        "r": (n((256, 1024))).astype(np.float32),
    }


def reference(x, xt, g, gt, r):
    x_ = mxq(f64(x), 0, "e4m3")
    xt_ = mxq(f64(xt), 0, "e4m3")
    g_ = mxq(f64(g), 0, "e5m2")
    gt_ = mxq(f64(gt), 0, "e5m2")
    y = x_.T @ xt_
    u = g_.T @ gt_
    y = y * u
    return f64(r) + y

@@ -1,0 +1,166 @@
+from contextlib import ExitStack
+
+import concourse.mybir as mybir
+
+K, M, N = 1536, 256, 1024
+FLOPS = 2 * 2 * K * M * N
+
+F32 = mybir.dt.float32
+BF16 = mybir.dt.bfloat16
+U32 = mybir.dt.uint32
+U8 = mybir.dt.uint8
+E4M3X4 = mybir.dt.float8_e4m3fn_x4
+E5M2X4 = mybir.dt.float8_e5m2_x4
+MULT = mybir.AluOpType.mult
+ADD = mybir.AluOpType.add
+
+P = 128
+PACK = 4
+K_PASS = P * PACK
+PASSES = K // K_PASS
+HALF = N // 2
+QUARTER = N // 4
+
+
+def tile_mix_ghost_res_kernel(tc, x, xt, g, gt, r, out):
+    nc = tc.nc
+    with ExitStack() as ctx:
+        raw = ctx.enter_context(tc.tile_pool(name="raw", bufs=1))
+        keep = ctx.enter_context(tc.tile_pool(name="keep", bufs=1))
+        stage = ctx.enter_context(tc.tile_pool(name="stage", bufs=5))
+        psum = ctx.enter_context(tc.psum_pool(name="psum", bufs=1))
+        ctx.enter_context(tc.manual_schedule())
+
+        codes = {}
+        scales = {}
+        for name, width in (("g", M), ("gt", N), ("x", M), ("xt", N)):
+            codes[name] = keep.tile([P, PASSES, width], U32, name=name + "_codes", align_bytes=64)
+            scales[name] = keep.tile([P, PASSES, width], U8, name=name + "_scales", align_bytes=64)
+        fmt = {"g": E5M2X4, "gt": E5M2X4, "x": E4M3X4, "xt": E4M3X4}
+
+        def load(name, src, c0, c1, lo, hi):
+            passes = c1 - c0
+            t = raw.tile([P, passes, PACK, hi - lo], F32, name="raw_%s_%d_%d" % (name, c0, lo), align_bytes=64)
+            for c in range(passes) if hi - lo < src.shape[1] else ():
+                nc.sync.dma_start(out=t[:, c], in_=src[(c0 + c) * K_PASS:(c0 + c + 1) * K_PASS, lo:hi].rearrange("(p j) w -> p j w", j=PACK))
+            if hi - lo == src.shape[1]:
+                nc.sync.dma_start(out=t[:], in_=src[c0 * K_PASS:c1 * K_PASS, :].rearrange("(c p j) w -> p c j w", c=passes, j=PACK))
+            return t
+
+        def interleave(src, cut):
+            width = src.shape[2]
+            grouped = stage.tile([P, HALF, PACK], BF16, name="grouped", align_bytes=64)
+            nc.scalar.copy(out=grouped[:, cut:width, :], in_=src[:, :, cut:width].rearrange("p j w -> p w j"))
+            nc.vector.tensor_copy(out=grouped[:, 0:cut, :], in_=src[:, :, 0:cut].rearrange("p j w -> p w j"))
+            return grouped
+
+        def quantize(name, c, lo, width, grouped):
+            nc.vector.quantize_mx(
+                out=codes[name][:, c, lo:lo + width].bitcast(fmt[name]),
+                scales=scales[name][:, c, lo:lo + width],
+                in_=grouped[:, 0:width, :].rearrange("p w j -> p (w j)"),
+            )
+
+        def matmul(acc, a, b, c, m, lo, width):
+            ms = slice(m * P, (m + 1) * P)
+            ns = slice(lo, lo + width)
+            nc.tensor.matmul_mx(
+                out=acc[:, 0:width],
+                lhsT=codes[a][:, c, ms].bitcast(fmt[a]),
+                lhsT_scale=scales[a][:, c, ms],
+                rhs=codes[b][:, c, ns].bitcast(fmt[b]),
+                rhs_scale=scales[b][:, c, ns],
+                start=(c == 0),
+                stop=(c == PASSES - 1),
+            )
+
+        g_raw0 = load("g", g, 0, 1, 0, M)
+        gt_raw = [load("gt", gt, 0, 1, 0, N)]
+        g_raw12 = load("g", g, 1, 3, 0, M)
+        gt_raw.append(load("gt", gt, 1, 2, 0, N))
+        gt_raw.append(load("gt", gt, 2, 3, 0, N))
+        x_raw = load("x", x, 0, 3, 0, M)
+        xt_raw0 = load("xt", xt, 0, 1, 0, N)
+        xt_h0 = load("xt", xt, 1, 3, 0, HALF)
+        r_sb = keep.tile([P, 2, N], F32, name="r_sb", align_bytes=64)
+        r_view = r.rearrange("(m p) n -> p m n", p=P)
+        out_view = out.rearrange("(m p) n -> p m n", p=P)
+        nc.sync.dma_start(out=r_sb[:, :, 0:HALF], in_=r_view[:, :, 0:HALF])
+        xt_h1 = load("xt", xt, 1, 2, HALF, N)
+        xt_q2 = load("xt", xt, 2, 3, HALF, HALF + QUARTER)
+        xt_q3 = load("xt", xt, 2, 3, HALF + QUARTER, N)
+        nc.sync.dma_start(out=r_sb[:, :, HALF:N], in_=r_view[:, :, HALF:N])
+
+        u_sb = keep.tile([P, 2, N], F32, name="u_sb", align_bytes=64)
+        y_sb = keep.tile([P, 2, N], F32, name="y_sb", align_bytes=64)
+
+        u_acc = [[psum.tile([P, HALF], F32, name="bank%d" % (2 * m + h)) for h in range(2)] for m in range(2)]
+        quantize("g", 0, 0, M, interleave(g_raw0[:, 0], 96))
+        for c in range(PASSES):
+            halves = [interleave(gt_raw[c][:, 0, :, h * HALF:(h + 1) * HALF], 192) for h in range(2)]
+            for h in range(2):
+                quantize("gt", c, h * HALF, HALF, halves[h])
+                for m in range(2):
+                    matmul(u_acc[m][h], "g", "gt", c, m, h * HALF, HALF)
+            if c == 0:
+                pair = [interleave(g_raw12[:, i], 96) for i in range(2)]
+                for i in range(2):
+                    quantize("g", 1 + i, 0, M, pair[i])
+        xs = [interleave(x_raw[:, c], 96) for c in range(PASSES)]
+        for h in range(2):
+            for m in range(2):
+                nc.scalar.copy(out=u_sb[:, m, h * HALF:(h + 1) * HALF], in_=u_acc[m][h][:])
+        for c in range(PASSES):
+            quantize("x", c, 0, M, xs[c])
+
+        a_h0 = [psum.tile([P, HALF], F32, name="bank%d" % (4 + m)) for m in range(2)]
+        a_q2 = [psum.tile([P, HALF], F32, name="bank%d" % (6 + m)) for m in range(2)]
+        a_q3 = [psum.tile([P, HALF], F32, name="bank%d" % m) for m in range(2)]
+
+        def multiply(acc, m, lo, width):
+            nc.vector.tensor_tensor(out=y_sb[:, m, lo:lo + width], in0=acc[m][:, 0:width], in1=u_sb[:, m, lo:lo + width], op=MULT)
+
+        def add_r(m, lo, width):
+            nc.vector.tensor_tensor(out=y_sb[:, m, lo:lo + width], in0=y_sb[:, m, lo:lo + width], in1=r_sb[:, m, lo:lo + width], op=ADD)
+
+        def store(m, lo, width):
+            nc.sync.dma_start(out=out_view[:, m, lo:lo + width], in_=y_sb[:, m, lo:lo + width])
+
+        Q2, Q3 = HALF, HALF + QUARTER
+        halves = [interleave(xt_raw0[:, 0, :, h * HALF:(h + 1) * HALF], 192) for h in range(2)]
+        for h in range(2):
+            quantize("xt", 0, h * HALF, HALF, halves[h])
+        for m in range(2):
+            matmul(a_h0[m], "x", "xt", 0, m, 0, HALF)
+        for m in range(2):
+            matmul(a_q2[m], "x", "xt", 0, m, Q2, QUARTER)
+            matmul(a_q3[m], "x", "xt", 0, m, Q3, QUARTER)
+        for c in (1, 2):
+            quantize("xt", c, 0, HALF, interleave(xt_h0[:, c - 1], 192))
+            for m in range(2):
+                matmul(a_h0[m], "x", "xt", c, m, 0, HALF)
+        h1 = interleave(xt_h1[:, 0], 96)
+        for m in range(2):
+            multiply(a_h0, m, 0, HALF)
+        for m in range(2):
+            add_r(m, 0, HALF)
+            store(m, 0, HALF)
+        q2 = interleave(xt_q2[:, 0], 96)
+        quantize("xt", 1, HALF, HALF, h1)
+        for m in range(2):
+            matmul(a_q2[m], "x", "xt", 1, m, Q2, QUARTER)
+            matmul(a_q3[m], "x", "xt", 1, m, Q3, QUARTER)
+        quantize("xt", 2, Q2, QUARTER, q2)
+        for m in range(2):
+            matmul(a_q2[m], "x", "xt", 2, m, Q2, QUARTER)
+        q3 = interleave(xt_q3[:, 0], 128)
+        quantize("xt", 2, Q3, QUARTER, q3)
+        for m in range(2):
+            matmul(a_q3[m], "x", "xt", 2, m, Q3, QUARTER)
+        for m in range(2):
+            multiply(a_q2, m, Q2, QUARTER)
+        for m in range(2):
+            multiply(a_q3, m, Q3, QUARTER)
+        for m in range(2):
+            add_r(m, HALF, HALF)
+            store(m, HALF, HALF)

@@ -50,8 +50,11 @@ def tile_mix_ghost_res_kernel(tc, x, xt, g, gt, r, out):
         def interleave(src, cut):
             width = src.shape[2]
             grouped = stage.tile([P, HALF, PACK], BF16, name="grouped", align_bytes=64)
-            nc.scalar.copy(out=grouped[:, cut:width, :], in_=src[:, :, cut:width].rearrange("p j w -> p w j"))
-            nc.vector.tensor_copy(out=grouped[:, 0:cut, :], in_=src[:, :, 0:cut].rearrange("p j w -> p w j"))
+            for copy, lo, hi in ((nc.scalar.copy, cut, width), (nc.vector.tensor_copy, 0, cut)):
+                copy(
+                    out=grouped[:, lo:hi, :].rearrange("p (b i) j -> p b j i", i=4),
+                    in_=src[:, :, lo:hi].rearrange("p j (b i) -> p b j i", i=4),
+                )
             return grouped
 
         def quantize(name, c, lo, width, grouped):
@@ -80,87 +83,93 @@ def tile_mix_ghost_res_kernel(tc, x, xt, g, gt, r, out):
         gt_raw.append(load("gt", gt, 1, 2, 0, N))
         gt_raw.append(load("gt", gt, 2, 3, 0, N))
         x_raw = load("x", x, 0, 3, 0, M)
-        xt_raw0 = load("xt", xt, 0, 1, 0, N)
-        xt_h0 = load("xt", xt, 1, 3, 0, HALF)
+        BLOCKS = ((0, 512), (512, 256), (768, 256))
+        FIRST, SECOND, THIRD = 0, 1, 2
         r_sb = keep.tile([P, 2, N], F32, name="r_sb", align_bytes=64)
         r_view = r.rearrange("(m p) n -> p m n", p=P)
         out_view = out.rearrange("(m p) n -> p m n", p=P)
-        nc.sync.dma_start(out=r_sb[:, :, 0:HALF], in_=r_view[:, :, 0:HALF])
-        xt_h1 = load("xt", xt, 1, 2, HALF, N)
-        xt_q2 = load("xt", xt, 2, 3, HALF, HALF + QUARTER)
-        xt_q3 = load("xt", xt, 2, 3, HALF + QUARTER, N)
+        xt_raw = []
+        for lo, width in BLOCKS:
+            xt_raw.append([load("xt", xt, c, c + 1, lo, lo + width) for c in range(PASSES)])
+            if lo == 0:
+                nc.sync.dma_start(out=r_sb[:, :, 0:HALF], in_=r_view[:, :, 0:HALF])
         nc.sync.dma_start(out=r_sb[:, :, HALF:N], in_=r_view[:, :, HALF:N])
 
         u_sb = keep.tile([P, 2, N], F32, name="u_sb", align_bytes=64)
         y_sb = keep.tile([P, 2, N], F32, name="y_sb", align_bytes=64)
 
         u_acc = [[psum.tile([P, HALF], F32, name="bank%d" % (2 * m + h)) for h in range(2)] for m in range(2)]
-        quantize("g", 0, 0, M, interleave(g_raw0[:, 0], 96))
+        quantize("g", 0, 0, M, interleave(g_raw0[:, 0], 128))
         for c in range(PASSES):
-            halves = [interleave(gt_raw[c][:, 0, :, h * HALF:(h + 1) * HALF], 192) for h in range(2)]
+            halves = [interleave(gt_raw[c][:, 0, :, h * HALF:(h + 1) * HALF], 256) for h in range(2)]
             for h in range(2):
                 quantize("gt", c, h * HALF, HALF, halves[h])
                 for m in range(2):
                     matmul(u_acc[m][h], "g", "gt", c, m, h * HALF, HALF)
             if c == 0:
-                pair = [interleave(g_raw12[:, i], 96) for i in range(2)]
+                pair = [interleave(g_raw12[:, i], 128) for i in range(2)]
                 for i in range(2):
                     quantize("g", 1 + i, 0, M, pair[i])
-        xs = [interleave(x_raw[:, c], 96) for c in range(PASSES)]
-        for h in range(2):
-            for m in range(2):
-                nc.scalar.copy(out=u_sb[:, m, h * HALF:(h + 1) * HALF], in_=u_acc[m][h][:])
+        xs = [interleave(x_raw[:, c], 128) for c in range(PASSES)]
         for c in range(PASSES):
             quantize("x", c, 0, M, xs[c])
 
-        a_h0 = [psum.tile([P, HALF], F32, name="bank%d" % (4 + m)) for m in range(2)]
-        a_q2 = [psum.tile([P, HALF], F32, name="bank%d" % (6 + m)) for m in range(2)]
-        a_q3 = [psum.tile([P, HALF], F32, name="bank%d" % m) for m in range(2)]
+        a_acc = [[psum.tile([P, HALF], F32, name="bank%d" % (b % 4 if b < 4 else b)) for b in bs] for bs in ((4, 5), (6, 7), (0, 2))]
+        grouped_xt = {}
 
-        def multiply(acc, m, lo, width):
-            nc.vector.tensor_tensor(out=y_sb[:, m, lo:lo + width], in0=acc[m][:, 0:width], in1=u_sb[:, m, lo:lo + width], op=MULT)
+        def cast(b, c):
+            grouped_xt[b, c] = interleave(xt_raw[b][c][:, 0], (256, 64, 96)[b])
 
-        def add_r(m, lo, width):
-            nc.vector.tensor_tensor(out=y_sb[:, m, lo:lo + width], in0=y_sb[:, m, lo:lo + width], in1=r_sb[:, m, lo:lo + width], op=ADD)
-
-        def store(m, lo, width):
-            nc.sync.dma_start(out=out_view[:, m, lo:lo + width], in_=y_sb[:, m, lo:lo + width])
-
-        Q2, Q3 = HALF, HALF + QUARTER
-        halves = [interleave(xt_raw0[:, 0, :, h * HALF:(h + 1) * HALF], 192) for h in range(2)]
-        for h in range(2):
-            quantize("xt", 0, h * HALF, HALF, halves[h])
-        for m in range(2):
-            matmul(a_h0[m], "x", "xt", 0, m, 0, HALF)
-        for m in range(2):
-            matmul(a_q2[m], "x", "xt", 0, m, Q2, QUARTER)
-            matmul(a_q3[m], "x", "xt", 0, m, Q3, QUARTER)
-        for c in (1, 2):
-            quantize("xt", c, 0, HALF, interleave(xt_h0[:, c - 1], 192))
+        def multiply_pass(b, c):
+            lo, width = BLOCKS[b]
+            quantize("xt", c, lo, width, grouped_xt[b, c])
             for m in range(2):
-                matmul(a_h0[m], "x", "xt", c, m, 0, HALF)
-        h1 = interleave(xt_h1[:, 0], 96)
-        for m in range(2):
-            multiply(a_h0, m, 0, HALF)
-        for m in range(2):
-            add_r(m, 0, HALF)
-            store(m, 0, HALF)
-        q2 = interleave(xt_q2[:, 0], 96)
-        quantize("xt", 1, HALF, HALF, h1)
-        for m in range(2):
-            matmul(a_q2[m], "x", "xt", 1, m, Q2, QUARTER)
-            matmul(a_q3[m], "x", "xt", 1, m, Q3, QUARTER)
-        quantize("xt", 2, Q2, QUARTER, q2)
-        for m in range(2):
-            matmul(a_q2[m], "x", "xt", 2, m, Q2, QUARTER)
-        q3 = interleave(xt_q3[:, 0], 128)
-        quantize("xt", 2, Q3, QUARTER, q3)
-        for m in range(2):
-            matmul(a_q3[m], "x", "xt", 2, m, Q3, QUARTER)
-        for m in range(2):
-            multiply(a_q2, m, Q2, QUARTER)
-        for m in range(2):
-            multiply(a_q3, m, Q3, QUARTER)
-        for m in range(2):
-            add_r(m, HALF, HALF)
-            store(m, HALF, HALF)
+                matmul(a_acc[b][m], "x", "xt", c, m, lo, width)
+
+        def copy_u(m, h):
+            nc.scalar.copy(out=u_sb[:, m, h * HALF:(h + 1) * HALF], in_=u_acc[m][h][:])
+
+        def product(b, m):
+            lo, width = BLOCKS[b]
+            nc.vector.tensor_tensor(out=y_sb[:, m, lo:lo + width], in0=a_acc[b][m][:, 0:width], in1=u_sb[:, m, lo:lo + width], op=MULT)
+
+        def add_and_store(b, m):
+            lo, width = BLOCKS[b]
+            cols = slice(lo, lo + width)
+            nc.vector.tensor_tensor(out=y_sb[:, m, cols], in0=y_sb[:, m, cols], in1=r_sb[:, m, cols], op=ADD)
+            nc.sync.dma_start(out=out_view[:, m, cols], in_=y_sb[:, m, cols])
+
+        cast(0, 0)
+        copy_u(0, 0)
+        copy_u(1, 0)
+        multiply_pass(0, 0)
+        cast(0, 1)
+        multiply_pass(0, 1)
+        cast(0, 2)
+        copy_u(0, 1)
+        copy_u(1, 1)
+        multiply_pass(0, 2)
+        product(0, 0)
+        cast(1, 0)
+        product(0, 1)
+        multiply_pass(1, 0)
+        cast(1, 1)
+        add_and_store(0, 0)
+        multiply_pass(1, 1)
+        cast(1, 2)
+        add_and_store(0, 1)
+        multiply_pass(1, 2)
+        cast(2, 0)
+        product(1, 0)
+        multiply_pass(2, 0)
+        cast(2, 1)
+        product(1, 1)
+        multiply_pass(2, 1)
+        cast(2, 2)
+        multiply_pass(2, 2)
+        add_and_store(1, 0)
+        add_and_store(1, 1)
+        product(2, 0)
+        product(2, 1)
+        add_and_store(2, 0)
+        add_and_store(2, 1)

@@ -51,6 +51,8 @@ def tile_mix_ghost_res_kernel(tc, x, xt, g, gt, r, out):
             width = src.shape[2]
             grouped = stage.tile([P, HALF, PACK], BF16, name="grouped", align_bytes=64)
             for copy, lo, hi in ((nc.scalar.copy, cut, width), (nc.vector.tensor_copy, 0, cut)):
+                if lo == hi:
+                    continue
                 copy(
                     out=grouped[:, lo:hi, :].rearrange("p (b i) j -> p b j i", i=4),
                     in_=src[:, :, lo:hi].rearrange("p j (b i) -> p b j i", i=4),
@@ -83,17 +85,19 @@ def tile_mix_ghost_res_kernel(tc, x, xt, g, gt, r, out):
         gt_raw.append(load("gt", gt, 1, 2, 0, N))
         gt_raw.append(load("gt", gt, 2, 3, 0, N))
         x_raw = load("x", x, 0, 3, 0, M)
-        BLOCKS = ((0, 512), (512, 256), (768, 256))
-        FIRST, SECOND, THIRD = 0, 1, 2
+        xt_raw = {(0, 0): load("xt", xt, 0, 1, 0, N)}
+        for c in (1, 2):
+            xt_raw[c, 0] = load("xt", xt, c, c + 1, 0, HALF)
         r_sb = keep.tile([P, 2, N], F32, name="r_sb", align_bytes=64)
         r_view = r.rearrange("(m p) n -> p m n", p=P)
         out_view = out.rearrange("(m p) n -> p m n", p=P)
-        xt_raw = []
-        for lo, width in BLOCKS:
-            xt_raw.append([load("xt", xt, c, c + 1, lo, lo + width) for c in range(PASSES)])
-            if lo == 0:
-                nc.sync.dma_start(out=r_sb[:, :, 0:HALF], in_=r_view[:, :, 0:HALF])
+        for c in (1, 2):
+            xt_raw[c, 1] = load("xt", xt, c, c + 1, HALF, HALF + QUARTER)
+        nc.sync.dma_start(out=r_sb[:, :, 0:HALF], in_=r_view[:, :, 0:HALF])
+        for c in (1, 2):
+            xt_raw[c, 2] = load("xt", xt, c, c + 1, HALF + QUARTER, N)
         nc.sync.dma_start(out=r_sb[:, :, HALF:N], in_=r_view[:, :, HALF:N])
+        BLOCKS = ((0, 512), (512, 256), (768, 256))
 
         u_sb = keep.tile([P, 2, N], F32, name="u_sb", align_bytes=64)
         y_sb = keep.tile([P, 2, N], F32, name="y_sb", align_bytes=64)
@@ -117,14 +121,18 @@ def tile_mix_ghost_res_kernel(tc, x, xt, g, gt, r, out):
         a_acc = [[psum.tile([P, HALF], F32, name="bank%d" % (b % 4 if b < 4 else b)) for b in bs] for bs in ((4, 5), (6, 7), (0, 2))]
         grouped_xt = {}
 
-        def cast(b, c):
-            grouped_xt[b, c] = interleave(xt_raw[b][c][:, 0], (256, 64, 96)[b])
+        def cast(b, c, cut):
+            grouped_xt[b, c] = interleave(xt_raw[c, b][:, 0], cut)
+
+        def sums(b, c):
+            lo, width = BLOCKS[b]
+            for m in range(2):
+                matmul(a_acc[b][m], "x", "xt", c, m, lo, width)
 
         def multiply_pass(b, c):
             lo, width = BLOCKS[b]
             quantize("xt", c, lo, width, grouped_xt[b, c])
-            for m in range(2):
-                matmul(a_acc[b][m], "x", "xt", c, m, lo, width)
+            sums(b, c)
 
         def copy_u(m, h):
             nc.scalar.copy(out=u_sb[:, m, h * HALF:(h + 1) * HALF], in_=u_acc[m][h][:])
@@ -139,33 +147,32 @@ def tile_mix_ghost_res_kernel(tc, x, xt, g, gt, r, out):
             nc.vector.tensor_tensor(out=y_sb[:, m, cols], in0=y_sb[:, m, cols], in1=r_sb[:, m, cols], op=ADD)
             nc.sync.dma_start(out=out_view[:, m, cols], in_=y_sb[:, m, cols])
 
-        cast(0, 0)
         copy_u(0, 0)
+        halves = [interleave(xt_raw[0, 0][:, 0, :, h * HALF:(h + 1) * HALF], 320) for h in range(2)]
         copy_u(1, 0)
-        multiply_pass(0, 0)
-        cast(0, 1)
-        multiply_pass(0, 1)
-        cast(0, 2)
+        for h in range(2):
+            quantize("xt", 0, h * HALF, HALF, halves[h])
+        for b in range(3):
+            sums(b, 0)
+        cast(0, 1, 320)
         copy_u(0, 1)
+        multiply_pass(0, 1)
+        cast(0, 2, 384)
         copy_u(1, 1)
         multiply_pass(0, 2)
+        cast(1, 1, 0)
         product(0, 0)
-        cast(1, 0)
         product(0, 1)
-        multiply_pass(1, 0)
-        cast(1, 1)
-        add_and_store(0, 0)
         multiply_pass(1, 1)
-        cast(1, 2)
-        add_and_store(0, 1)
+        cast(1, 2, 0)
         multiply_pass(1, 2)
-        cast(2, 0)
+        add_and_store(0, 0)
         product(1, 0)
-        multiply_pass(2, 0)
-        cast(2, 1)
+        add_and_store(0, 1)
         product(1, 1)
+        cast(2, 1, 0)
+        cast(2, 2, 128)
         multiply_pass(2, 1)
-        cast(2, 2)
         multiply_pass(2, 2)
         add_and_store(1, 0)
         add_and_store(1, 1)

@@ -3,7 +3,7 @@ from contextlib import ExitStack
 import concourse.mybir as mybir
 
 K, M, N = 1536, 256, 1024
-FLOPS = 2 * 2 * K * M * N
+FLOPS = 2 * (2 * K * M * N)
 
 F32 = mybir.dt.float32
 BF16 = mybir.dt.bfloat16
@@ -18,8 +18,11 @@ P = 128
 PACK = 4
 K_PASS = P * PACK
 PASSES = K // K_PASS
+CAST_RUN = 4
+M_TILES = M // P
 HALF = N // 2
-QUARTER = N // 4
+
+STRIPS = ((0, HALF), (HALF, HALF // 2), (HALF + HALF // 2, HALF // 2))
 
 
 def tile_mix_ghost_res_kernel(tc, x, xt, g, gt, r, out):
@@ -31,152 +34,141 @@ def tile_mix_ghost_res_kernel(tc, x, xt, g, gt, r, out):
         psum = ctx.enter_context(tc.psum_pool(name="psum", bufs=1))
         ctx.enter_context(tc.manual_schedule())
 
+        formats = {"x": E4M3X4, "xt": E4M3X4, "g": E5M2X4, "gt": E5M2X4}
         codes = {}
         scales = {}
         for name, width in (("g", M), ("gt", N), ("x", M), ("xt", N)):
             codes[name] = keep.tile([P, PASSES, width], U32, name=name + "_codes", align_bytes=64)
             scales[name] = keep.tile([P, PASSES, width], U8, name=name + "_scales", align_bytes=64)
-        fmt = {"g": E5M2X4, "gt": E5M2X4, "x": E4M3X4, "xt": E4M3X4}
 
-        def load(name, src, c0, c1, lo, hi):
-            passes = c1 - c0
-            t = raw.tile([P, passes, PACK, hi - lo], F32, name="raw_%s_%d_%d" % (name, c0, lo), align_bytes=64)
-            for c in range(passes) if hi - lo < src.shape[1] else ():
-                nc.sync.dma_start(out=t[:, c], in_=src[(c0 + c) * K_PASS:(c0 + c + 1) * K_PASS, lo:hi].rearrange("(p j) w -> p j w", j=PACK))
-            if hi - lo == src.shape[1]:
-                nc.sync.dma_start(out=t[:], in_=src[c0 * K_PASS:c1 * K_PASS, :].rearrange("(c p j) w -> p c j w", c=passes, j=PACK))
-            return t
+        def load(name, src, first, count, lo, width):
+            tile = raw.tile([P, count, PACK, width], F32, name="raw_%s_%d_%d" % (name, first, lo), align_bytes=64)
+            rows = src[first * K_PASS : (first + count) * K_PASS, lo : lo + width]
+            nc.sync.dma_start(out=tile[:], in_=rows.rearrange("(c p j) w -> p c j w", c=count, j=PACK))
+            return tile
 
-        def interleave(src, cut):
+        def cast(src, vector_columns):
             width = src.shape[2]
-            grouped = stage.tile([P, HALF, PACK], BF16, name="grouped", align_bytes=64)
-            for copy, lo, hi in ((nc.scalar.copy, cut, width), (nc.vector.tensor_copy, 0, cut)):
-                if lo == hi:
-                    continue
-                copy(
-                    out=grouped[:, lo:hi, :].rearrange("p (b i) j -> p b j i", i=4),
-                    in_=src[:, :, lo:hi].rearrange("p j (b i) -> p b j i", i=4),
-                )
-            return grouped
+            tile = stage.tile([P, HALF, PACK], BF16, name="grouped", align_bytes=64)
+            for copy, lo, hi in ((nc.scalar.copy, vector_columns, width), (nc.vector.tensor_copy, 0, vector_columns)):
+                if hi > lo:
+                    copy(
+                        out=tile[:, lo:hi, :].rearrange("p (b i) j -> p b j i", i=CAST_RUN),
+                        in_=src[:, :, lo:hi].rearrange("p j (b i) -> p b j i", i=CAST_RUN),
+                    )
+            return tile
 
         def quantize(name, c, lo, width, grouped):
             nc.vector.quantize_mx(
-                out=codes[name][:, c, lo:lo + width].bitcast(fmt[name]),
-                scales=scales[name][:, c, lo:lo + width],
+                out=codes[name][:, c, lo : lo + width].bitcast(formats[name]),
+                scales=scales[name][:, c, lo : lo + width],
                 in_=grouped[:, 0:width, :].rearrange("p w j -> p (w j)"),
             )
 
-        def matmul(acc, a, b, c, m, lo, width):
-            ms = slice(m * P, (m + 1) * P)
-            ns = slice(lo, lo + width)
+        def multiply(acc, stationary, moving, c, m, lo, width):
+            rows = slice(m * P, (m + 1) * P)
+            cols = slice(lo, lo + width)
             nc.tensor.matmul_mx(
                 out=acc[:, 0:width],
-                lhsT=codes[a][:, c, ms].bitcast(fmt[a]),
-                lhsT_scale=scales[a][:, c, ms],
-                rhs=codes[b][:, c, ns].bitcast(fmt[b]),
-                rhs_scale=scales[b][:, c, ns],
+                lhsT=codes[stationary][:, c, rows].bitcast(formats[stationary]),
+                lhsT_scale=scales[stationary][:, c, rows],
+                rhs=codes[moving][:, c, cols].bitcast(formats[moving]),
+                rhs_scale=scales[moving][:, c, cols],
                 start=(c == 0),
                 stop=(c == PASSES - 1),
             )
 
-        g_raw0 = load("g", g, 0, 1, 0, M)
+        g_first = load("g", g, 0, 1, 0, M)
         gt_raw = [load("gt", gt, 0, 1, 0, N)]
-        g_raw12 = load("g", g, 1, 3, 0, M)
-        gt_raw.append(load("gt", gt, 1, 2, 0, N))
-        gt_raw.append(load("gt", gt, 2, 3, 0, N))
-        x_raw = load("x", x, 0, 3, 0, M)
-        xt_raw = {(0, 0): load("xt", xt, 0, 1, 0, N)}
-        for c in (1, 2):
-            xt_raw[c, 0] = load("xt", xt, c, c + 1, 0, HALF)
-        r_sb = keep.tile([P, 2, N], F32, name="r_sb", align_bytes=64)
-        r_view = r.rearrange("(m p) n -> p m n", p=P)
-        out_view = out.rearrange("(m p) n -> p m n", p=P)
-        for c in (1, 2):
-            xt_raw[c, 1] = load("xt", xt, c, c + 1, HALF, HALF + QUARTER)
-        nc.sync.dma_start(out=r_sb[:, :, 0:HALF], in_=r_view[:, :, 0:HALF])
-        for c in (1, 2):
-            xt_raw[c, 2] = load("xt", xt, c, c + 1, HALF + QUARTER, N)
-        nc.sync.dma_start(out=r_sb[:, :, HALF:N], in_=r_view[:, :, HALF:N])
-        BLOCKS = ((0, 512), (512, 256), (768, 256))
+        g_rest = load("g", g, 1, PASSES - 1, 0, M)
+        gt_raw += [load("gt", gt, c, 1, 0, N) for c in range(1, PASSES)]
+        x_raw = load("x", x, 0, PASSES, 0, M)
+        xt_first = load("xt", xt, 0, 1, 0, N)
+        xt_raw = {(0, c): load("xt", xt, c, 1, *STRIPS[0]) for c in range(1, PASSES)}
+        r_sb = keep.tile([P, M_TILES, N], F32, name="r_sb", align_bytes=64)
+        r_rows = r.rearrange("(m p) n -> p m n", p=P)
+        out_rows = out.rearrange("(m p) n -> p m n", p=P)
+        for s in (1, 2):
+            for c in range(1, PASSES):
+                xt_raw[s, c] = load("xt", xt, c, 1, *STRIPS[s])
+            r_cols = slice((s - 1) * HALF, s * HALF)
+            nc.sync.dma_start(out=r_sb[:, :, r_cols], in_=r_rows[:, :, r_cols])
+        u_sb = keep.tile([P, M_TILES, N], F32, name="u_sb", align_bytes=64)
+        y_sb = keep.tile([P, M_TILES, N], F32, name="y_sb", align_bytes=64)
 
-        u_sb = keep.tile([P, 2, N], F32, name="u_sb", align_bytes=64)
-        y_sb = keep.tile([P, 2, N], F32, name="y_sb", align_bytes=64)
+        u_acc = [[psum.tile([P, HALF], F32, name="bank%d" % (2 * m + h)) for h in range(2)] for m in range(M_TILES)]
 
-        u_acc = [[psum.tile([P, HALF], F32, name="bank%d" % (2 * m + h)) for h in range(2)] for m in range(2)]
-        quantize("g", 0, 0, M, interleave(g_raw0[:, 0], 128))
+        def prepare_narrow(name, tile, first, count):
+            grouped = [cast(tile[:, i], M // 2) for i in range(count)]
+            for i in range(count):
+                quantize(name, first + i, 0, M, grouped[i])
+
+        prepare_narrow("g", g_first, 0, 1)
         for c in range(PASSES):
-            halves = [interleave(gt_raw[c][:, 0, :, h * HALF:(h + 1) * HALF], 256) for h in range(2)]
+            grouped = [cast(gt_raw[c][:, 0, :, h * HALF : (h + 1) * HALF], HALF // 2) for h in range(2)]
             for h in range(2):
-                quantize("gt", c, h * HALF, HALF, halves[h])
-                for m in range(2):
-                    matmul(u_acc[m][h], "g", "gt", c, m, h * HALF, HALF)
+                quantize("gt", c, h * HALF, HALF, grouped[h])
+                for m in range(M_TILES):
+                    multiply(u_acc[m][h], "g", "gt", c, m, h * HALF, HALF)
             if c == 0:
-                pair = [interleave(g_raw12[:, i], 128) for i in range(2)]
-                for i in range(2):
-                    quantize("g", 1 + i, 0, M, pair[i])
-        xs = [interleave(x_raw[:, c], 128) for c in range(PASSES)]
-        for c in range(PASSES):
-            quantize("x", c, 0, M, xs[c])
+                prepare_narrow("g", g_rest, 1, PASSES - 1)
 
-        a_acc = [[psum.tile([P, HALF], F32, name="bank%d" % (b % 4 if b < 4 else b)) for b in bs] for bs in ((4, 5), (6, 7), (0, 2))]
-        grouped_xt = {}
+        prepare_narrow("x", x_raw, 0, PASSES)
+        a_acc = [[psum.tile([P, HALF], F32, name="bank%d" % bank) for bank in banks] for banks in ((4, 5), (6, 7), (0, 2))]
 
-        def cast(b, c, cut):
-            grouped_xt[b, c] = interleave(xt_raw[c, b][:, 0], cut)
+        def keep_u(m, h):
+            nc.scalar.copy(out=u_sb[:, m, h * HALF : (h + 1) * HALF], in_=u_acc[m][h][:])
 
-        def sums(b, c):
-            lo, width = BLOCKS[b]
-            for m in range(2):
-                matmul(a_acc[b][m], "x", "xt", c, m, lo, width)
+        def multiply_strip(s, c):
+            lo, width = STRIPS[s]
+            for m in range(M_TILES):
+                multiply(a_acc[s][m], "x", "xt", c, m, lo, width)
 
-        def multiply_pass(b, c):
-            lo, width = BLOCKS[b]
-            quantize("xt", c, lo, width, grouped_xt[b, c])
-            sums(b, c)
+        def quantize_strip(s, c, grouped_strip):
+            lo, width = STRIPS[s]
+            quantize("xt", c, lo, width, grouped_strip)
+            multiply_strip(s, c)
 
-        def copy_u(m, h):
-            nc.scalar.copy(out=u_sb[:, m, h * HALF:(h + 1) * HALF], in_=u_acc[m][h][:])
+        def product(s, m):
+            lo, width = STRIPS[s]
+            cols = slice(lo, lo + width)
+            nc.vector.tensor_tensor(out=y_sb[:, m, cols], in0=a_acc[s][m][:, 0:width], in1=u_sb[:, m, cols], op=MULT)
 
-        def product(b, m):
-            lo, width = BLOCKS[b]
-            nc.vector.tensor_tensor(out=y_sb[:, m, lo:lo + width], in0=a_acc[b][m][:, 0:width], in1=u_sb[:, m, lo:lo + width], op=MULT)
-
-        def add_and_store(b, m):
-            lo, width = BLOCKS[b]
+        def finish(s, m):
+            lo, width = STRIPS[s]
             cols = slice(lo, lo + width)
             nc.vector.tensor_tensor(out=y_sb[:, m, cols], in0=y_sb[:, m, cols], in1=r_sb[:, m, cols], op=ADD)
-            nc.sync.dma_start(out=out_view[:, m, cols], in_=y_sb[:, m, cols])
+            nc.sync.dma_start(out=out_rows[:, m, cols], in_=y_sb[:, m, cols])
 
-        copy_u(0, 0)
-        halves = [interleave(xt_raw[0, 0][:, 0, :, h * HALF:(h + 1) * HALF], 320) for h in range(2)]
-        copy_u(1, 0)
+        keep_u(0, 0)
+        grouped = [cast(xt_first[:, 0, :, h * HALF : (h + 1) * HALF], 320) for h in range(2)]
+        keep_u(1, 0)
         for h in range(2):
-            quantize("xt", 0, h * HALF, HALF, halves[h])
-        for b in range(3):
-            sums(b, 0)
-        cast(0, 1, 320)
-        copy_u(0, 1)
-        multiply_pass(0, 1)
-        cast(0, 2, 384)
-        copy_u(1, 1)
-        multiply_pass(0, 2)
-        cast(1, 1, 0)
-        product(0, 0)
-        product(0, 1)
-        multiply_pass(1, 1)
-        cast(1, 2, 0)
-        multiply_pass(1, 2)
-        add_and_store(0, 0)
-        product(1, 0)
-        add_and_store(0, 1)
-        product(1, 1)
-        cast(2, 1, 0)
-        cast(2, 2, 128)
-        multiply_pass(2, 1)
-        multiply_pass(2, 2)
-        add_and_store(1, 0)
-        add_and_store(1, 1)
-        product(2, 0)
-        product(2, 1)
-        add_and_store(2, 0)
-        add_and_store(2, 1)
+            quantize("xt", 0, h * HALF, HALF, grouped[h])
+        for s in range(len(STRIPS)):
+            multiply_strip(s, 0)
+        grouped = cast(xt_raw[0, 1][:, 0], 320)
+        keep_u(0, 1)
+        quantize_strip(0, 1, grouped)
+        grouped = cast(xt_raw[0, 2][:, 0], 384)
+        keep_u(1, 1)
+        quantize_strip(0, 2, grouped)
+
+        grouped = cast(xt_raw[1, 1][:, 0], 0)
+        for m in range(M_TILES):
+            product(0, m)
+        quantize_strip(1, 1, grouped)
+        quantize_strip(1, 2, cast(xt_raw[1, 2][:, 0], 0))
+        for m in range(M_TILES):
+            finish(0, m)
+            product(1, m)
+
+        grouped = [cast(xt_raw[2, 1][:, 0], 0), cast(xt_raw[2, 2][:, 0], 128)]
+        for c in range(1, PASSES):
+            quantize_strip(2, c, grouped[c - 1])
+        for m in range(M_TILES):
+            finish(1, m)
+        for m in range(M_TILES):
+            product(2, m)
+        for m in range(M_TILES):
+            finish(2, m)

from contextlib import ExitStack

import concourse.mybir as mybir

K, M, N = 1536, 256, 1024
FLOPS = 2 * (2 * K * M * N)

F32 = mybir.dt.float32
BF16 = mybir.dt.bfloat16
U32 = mybir.dt.uint32
U8 = mybir.dt.uint8
E4M3X4 = mybir.dt.float8_e4m3fn_x4
E5M2X4 = mybir.dt.float8_e5m2_x4
MULT = mybir.AluOpType.mult
ADD = mybir.AluOpType.add

P = 128
PACK = 4
K_PASS = P * PACK
PASSES = K // K_PASS
CAST_RUN = 4
M_TILES = M // P
HALF = N // 2

STRIPS = ((0, HALF), (HALF, HALF // 2), (HALF + HALF // 2, HALF // 2))


def tile_mix_ghost_res_kernel(tc, x, xt, g, gt, r, out):
    nc = tc.nc
    with ExitStack() as ctx:
        raw = ctx.enter_context(tc.tile_pool(name="raw", bufs=1))
        keep = ctx.enter_context(tc.tile_pool(name="keep", bufs=1))
        stage = ctx.enter_context(tc.tile_pool(name="stage", bufs=5))
        psum = ctx.enter_context(tc.psum_pool(name="psum", bufs=1))
        ctx.enter_context(tc.manual_schedule())

        formats = {"x": E4M3X4, "xt": E4M3X4, "g": E5M2X4, "gt": E5M2X4}
        codes = {}
        scales = {}
        for name, width in (("g", M), ("gt", N), ("x", M), ("xt", N)):
            codes[name] = keep.tile([P, PASSES, width], U32, name=name + "_codes", align_bytes=64)
            scales[name] = keep.tile([P, PASSES, width], U8, name=name + "_scales", align_bytes=64)

        def load(name, src, first, count, lo, width):
            tile = raw.tile([P, count, PACK, width], F32, name="raw_%s_%d_%d" % (name, first, lo), align_bytes=64)
            rows = src[first * K_PASS : (first + count) * K_PASS, lo : lo + width]
            nc.sync.dma_start(out=tile[:], in_=rows.rearrange("(c p j) w -> p c j w", c=count, j=PACK))
            return tile

        def cast(src, vector_columns):
            width = src.shape[2]
            tile = stage.tile([P, HALF, PACK], BF16, name="grouped", align_bytes=64)
            for copy, lo, hi in ((nc.scalar.copy, vector_columns, width), (nc.vector.tensor_copy, 0, vector_columns)):
                if hi > lo:
                    copy(
                        out=tile[:, lo:hi, :].rearrange("p (b i) j -> p b j i", i=CAST_RUN),
                        in_=src[:, :, lo:hi].rearrange("p j (b i) -> p b j i", i=CAST_RUN),
                    )
            return tile

        def quantize(name, c, lo, width, grouped):
            nc.vector.quantize_mx(
                out=codes[name][:, c, lo : lo + width].bitcast(formats[name]),
                scales=scales[name][:, c, lo : lo + width],
                in_=grouped[:, 0:width, :].rearrange("p w j -> p (w j)"),
            )

        def multiply(acc, stationary, moving, c, m, lo, width):
            rows = slice(m * P, (m + 1) * P)
            cols = slice(lo, lo + width)
            nc.tensor.matmul_mx(
                out=acc[:, 0:width],
                lhsT=codes[stationary][:, c, rows].bitcast(formats[stationary]),
                lhsT_scale=scales[stationary][:, c, rows],
                rhs=codes[moving][:, c, cols].bitcast(formats[moving]),
                rhs_scale=scales[moving][:, c, cols],
                start=(c == 0),
                stop=(c == PASSES - 1),
            )

        g_first = load("g", g, 0, 1, 0, M)
        gt_raw = [load("gt", gt, 0, 1, 0, N)]
        g_rest = load("g", g, 1, PASSES - 1, 0, M)
        gt_raw += [load("gt", gt, c, 1, 0, N) for c in range(1, PASSES)]
        x_raw = load("x", x, 0, PASSES, 0, M)
        xt_first = load("xt", xt, 0, 1, 0, N)
        xt_raw = {(0, c): load("xt", xt, c, 1, *STRIPS[0]) for c in range(1, PASSES)}
        r_sb = keep.tile([P, M_TILES, N], F32, name="r_sb", align_bytes=64)
        r_rows = r.rearrange("(m p) n -> p m n", p=P)
        out_rows = out.rearrange("(m p) n -> p m n", p=P)
        for s in (1, 2):
            for c in range(1, PASSES):
                xt_raw[s, c] = load("xt", xt, c, 1, *STRIPS[s])
            r_cols = slice((s - 1) * HALF, s * HALF)
            nc.sync.dma_start(out=r_sb[:, :, r_cols], in_=r_rows[:, :, r_cols])
        u_sb = keep.tile([P, M_TILES, N], F32, name="u_sb", align_bytes=64)
        y_sb = keep.tile([P, M_TILES, N], F32, name="y_sb", align_bytes=64)

        u_acc = [[psum.tile([P, HALF], F32, name="bank%d" % (2 * m + h)) for h in range(2)] for m in range(M_TILES)]

        def prepare_narrow(name, tile, first, count):
            grouped = [cast(tile[:, i], M // 2) for i in range(count)]
            for i in range(count):
                quantize(name, first + i, 0, M, grouped[i])

        prepare_narrow("g", g_first, 0, 1)
        for c in range(PASSES):
            grouped = [cast(gt_raw[c][:, 0, :, h * HALF : (h + 1) * HALF], HALF // 2) for h in range(2)]
            for h in range(2):
                quantize("gt", c, h * HALF, HALF, grouped[h])
                for m in range(M_TILES):
                    multiply(u_acc[m][h], "g", "gt", c, m, h * HALF, HALF)
            if c == 0:
                prepare_narrow("g", g_rest, 1, PASSES - 1)

        prepare_narrow("x", x_raw, 0, PASSES)
        a_acc = [[psum.tile([P, HALF], F32, name="bank%d" % bank) for bank in banks] for banks in ((4, 5), (6, 7), (0, 2))]

        def keep_u(m, h):
            nc.scalar.copy(out=u_sb[:, m, h * HALF : (h + 1) * HALF], in_=u_acc[m][h][:])

        def multiply_strip(s, c):
            lo, width = STRIPS[s]
            for m in range(M_TILES):
                multiply(a_acc[s][m], "x", "xt", c, m, lo, width)

        def quantize_strip(s, c, grouped_strip):
            lo, width = STRIPS[s]
            quantize("xt", c, lo, width, grouped_strip)
            multiply_strip(s, c)

        def product(s, m):
            lo, width = STRIPS[s]
            cols = slice(lo, lo + width)
            nc.vector.tensor_tensor(out=y_sb[:, m, cols], in0=a_acc[s][m][:, 0:width], in1=u_sb[:, m, cols], op=MULT)

        def finish(s, m):
            lo, width = STRIPS[s]
            cols = slice(lo, lo + width)
            nc.vector.tensor_tensor(out=y_sb[:, m, cols], in0=y_sb[:, m, cols], in1=r_sb[:, m, cols], op=ADD)
            nc.sync.dma_start(out=out_rows[:, m, cols], in_=y_sb[:, m, cols])

        keep_u(0, 0)
        grouped = [cast(xt_first[:, 0, :, h * HALF : (h + 1) * HALF], 320) for h in range(2)]
        keep_u(1, 0)
        for h in range(2):
            quantize("xt", 0, h * HALF, HALF, grouped[h])
        for s in range(len(STRIPS)):
            multiply_strip(s, 0)
        grouped = cast(xt_raw[0, 1][:, 0], 320)
        keep_u(0, 1)
        quantize_strip(0, 1, grouped)
        grouped = cast(xt_raw[0, 2][:, 0], 384)
        keep_u(1, 1)
        quantize_strip(0, 2, grouped)

        grouped = cast(xt_raw[1, 1][:, 0], 0)
        for m in range(M_TILES):
            product(0, m)
        quantize_strip(1, 1, grouped)
        quantize_strip(1, 2, cast(xt_raw[1, 2][:, 0], 0))
        for m in range(M_TILES):
            finish(0, m)
            product(1, m)

        grouped = [cast(xt_raw[2, 1][:, 0], 0), cast(xt_raw[2, 2][:, 0], 128)]
        for c in range(1, PASSES):
            quantize_strip(2, c, grouped[c - 1])
        for m in range(M_TILES):
            finish(1, m)
        for m in range(M_TILES):
            product(2, m)
        for m in range(M_TILES):
            finish(2, m)
